import numpy as np
import ml_dtypes


def mxq(x, axis, fmt="e4m3"):
    dtype, down = {"e4m3": (ml_dtypes.float8_e4m3fn, 7), "e5m2": (ml_dtypes.float8_e5m2, 14)}[fmt]
    v = np.moveaxis(np.asarray(x, np.float32).astype(ml_dtypes.bfloat16).astype(np.float64), axis, -1)
    blocks = v.reshape(v.shape[:-1] + (-1, 32))
    amax = np.abs(blocks).max(-1, keepdims=True)
    byte = np.maximum(np.where(amax > 0, np.frexp(amax)[1] - 1 + 127, 0) - down, 1)
    scale = np.exp2(byte - 127.0)
    codes = (blocks / scale).astype(np.float32).astype(dtype).astype(np.float64)
    return np.moveaxis((codes * scale).reshape(v.shape), -1, axis)


WIDE = False


def mx_kscale(k):
    if not WIDE:
        return np.ones(k)
    levels = np.array([30, -30])
    if k % 512:
        return np.exp2(np.random.permutation(np.resize(levels, k // 32))).repeat(32)
    a = np.empty((k // 512, 16))
    for p in range(k // 512):
        a[p, :8] = np.random.permutation(np.resize(levels, 8))
        for g in range(8):
            far = levels[np.abs(levels - a[p, g]) >= 10]
            a[p, g + 8] = far[np.random.randint(len(far))]
    return np.exp2(a.ravel()).repeat(32)


def f64(x):
    return np.asarray(x).astype(np.float64)


def striped(idx):
    return np.tile(np.asarray(idx).reshape(-1, 16).T, (8, 1)).astype(np.uint16)


def unstriped(offs):
    return offs[:16].T.reshape(-1).astype(np.int64)


E2M1 = np.array([0.0, 0.5, 1.0, 1.5, 2.0, 3.0, 4.0, 6.0, -0.0, -0.5, -1.0, -1.5, -2.0, -3.0, -4.0, -6.0])


def pack_weight(w, fmt):
    k, n = w.shape
    w = f64(np.asarray(w, np.float32).astype(ml_dtypes.bfloat16)).reshape(k // 32, 32, n)
    amax = np.abs(w).max(1)
    if fmt == "e4m3":
        byte = np.frexp(amax)[1] - 1 + 127 - 7
    else:
        mant, ex = np.frexp(amax / 6.0)
        byte = np.where(mant > 0.5, ex, ex - 1) + 127
    byte = np.clip(np.where(amax > 0, byte, 1), 1, 254)
    scaled = (w * np.exp2(127.0 - byte)[:, None, :]).reshape(k, n).astype(np.float32)
    by_word = np.ascontiguousarray(scaled.reshape(k // 512, 128, 4, n).transpose(0, 1, 3, 2))
    if fmt == "e4m3":
        words = by_word.astype(ml_dtypes.float8_e4m3fn).view(np.uint8)
    else:
        c = by_word.astype(ml_dtypes.float4_e2m1fn).view(np.uint8) & 0xF
        words = (c[..., 0::2] | (c[..., 1::2] << 4)).reshape(k // 512, 128, 2 * n)
    return np.ascontiguousarray(words), np.ascontiguousarray(byte.astype(np.uint8).reshape(k // 512, 16, n))


def unpack_weight(words, scales, fmt):
    g, _, n = scales.shape
    words = np.ascontiguousarray(words).reshape(g, 128, n, -1)
    if fmt == "e4m3":
        vals = words.view(ml_dtypes.float8_e4m3fn).astype(np.float64)
    else:
        nib = np.empty((g, 128, n, 4), np.uint8)
        nib[..., 0::2] = words & 0xF
        nib[..., 1::2] = words >> 4
        vals = E2M1[nib]
    vals = vals * np.repeat(np.exp2(scales.astype(np.float64) - 127.0), 8, axis=1)[..., None]
    return vals.transpose(0, 1, 3, 2).reshape(g * 512, n)


K, T, J, R, V, N = 512, 1024, 256, 512, 1024, 256


def setup_inputs():
    n = np.random.standard_normal
    idx = np.random.permutation(T)[:J]
    idx2 = np.random.permutation(V)[:J]
    idx3 = np.random.permutation(V)[:J]
    idx4 = np.random.permutation(T)[:J]
    fk = mx_kscale(K)
    fr = mx_kscale(R)
    xtp = pack_weight(n((K, T)) / fk[:, None], "e2m1")
    wp = pack_weight(n((K, R)) * 1 / np.sqrt(K) * fk[:, None] * fr, "e4m3")
    wbp = pack_weight(n((R, N)) * 1 / np.sqrt(R) / fr[:, None], "e2m1")
    wsp = pack_weight(n((K, N)) * 1 / np.sqrt(K) * fk[:, None], "e4m3")
    return {
        "xt_words": xtp[0],
        "xt_scales": xtp[1],
        "w_words": wp[0],
        "w_scales": wp[1],
        "tb": (np.random.randint(-9, 10, (R, V)).astype(np.float64)).astype(np.float32),
        "sa": (np.random.uniform(0.12, 0.3, (R, 1)) * fr[:, None]).astype(np.float32),
        "sb": (np.random.uniform(0.06, 0.2, (R, 1)) * fr[:, None]).astype(np.float32),
        "wb_words": wbp[0],
        "wb_scales": wbp[1],
        "ws_words": wsp[0],
        "ws_scales": wsp[1],
        "offs": striped(idx),
        "offs2": striped(idx2),
        "offs3": striped(idx3),
        "offs4": striped(idx4),
    }


def reference(xt_words, xt_scales, w_words, w_scales, tb, sa, sb, wb_words, wb_scales, ws_words, ws_scales, offs, offs2, offs3, offs4):
    idx = unstriped(offs)
    idx2 = unstriped(offs2)
    idx3 = unstriped(offs3)
    idx4 = unstriped(offs4)
    xtu = unpack_weight(xt_words, xt_scales, "e2m1")
    wu = unpack_weight(w_words, w_scales, "e4m3")
    wbu = unpack_weight(wb_words, wb_scales, "e2m1")
    wsu = unpack_weight(ws_words, ws_scales, "e4m3")
    xtidxg = xtu[:, idx]
    a = wu.T @ xtidxg
    hid = np.maximum(np.minimum(a, f64(tb)[:, idx2] * f64(sa)), f64(tb)[:, idx3] * f64(sb))
    hidq = mxq(hid, 0, "e5m2")
    xtidx4g = xtu[:, idx4]
    y = wbu.T @ hidq + wsu.T @ xtidx4g
    return y

from contextlib import ExitStack

import concourse.mybir as mybir

K, T, J, R, V, N = 512, 1024, 256, 512, 1024, 256
FLOPS = 2 * J * (K * R + R * N + K * N)

F32 = mybir.dt.float32
BF16 = mybir.dt.bfloat16
I32 = mybir.dt.int32
U32 = mybir.dt.uint32
U16 = mybir.dt.uint16
U8 = mybir.dt.uint8
E4M3 = mybir.dt.float8_e4m3fn_x4
E5M2 = mybir.dt.float8_e5m2_x4
E2M1 = mybir.dt.float4_e2m1fn_x4
ALU = mybir.AluOpType
COPY = mybir.ActivationFunctionType.Copy

P = 128
PACK = 4
HALF = J // 2
LIST_COLS = J // 16


def tile_list_twostepbounds_solo_further_plain_kernel(
    tc, xt_words, xt_scales, w_words, w_scales, tb, sa, sb, wb_words, wb_scales,
    ws_words, ws_scales, offs, offs2, offs3, offs4, out,
):
    nc = tc.nc
    with ExitStack() as ctx:
        keep = ctx.enter_context(tc.tile_pool(name="keep", bufs=1))
        psum = ctx.enter_context(tc.psum_pool(name="psum", bufs=1))

        def sbuf(name, shape, dtype):
            return keep.tile(shape, dtype, name=name, align_bytes=64)

        l1 = keep.tile([P, LIST_COLS], U16, name="l1")
        l2 = keep.tile([P, LIST_COLS], U16, name="l2")
        l3 = keep.tile([P, LIST_COLS], U16, name="l3")
        l4 = keep.tile([P, LIST_COLS], U16, name="l4")

        xs_stage = sbuf("xs_stage", [4, 4 * T], U8)
        xs_plane = sbuf("xs_plane", [P, T], U8)
        x_words = sbuf("x_words", [P, T], U16)
        w_raw = sbuf("w_raw", [P, R], U32)
        w_dealt = sbuf("w_dealt", [P, R], U32)
        wsc_raw = sbuf("wsc_raw", [P, 2 * R], U8)
        wsc_dealt = sbuf("wsc_dealt", [P, R], U8)
        osc = sbuf("osc", [P, 4 * N], U8)
        ws_sb = sbuf("ws_sb", [P, N], U32)
        wb_sb = sbuf("wb_sb", [P, 2 * N], U8)
        sa_sb = sbuf("sa_sb", [P, PACK], F32)
        sb_sb = sbuf("sb_sb", [P, PACK], F32)
        tb_sb = [sbuf("tb%d" % t, [P, V], F32) for t in range(PACK)]

        nc.vector.memset(wsc_raw[:].bitcast(I32), 0)
        nc.vector.memset(xs_plane[:].bitcast(I32), 0)
        nc.vector.memset(osc[:].bitcast(I32), 0)

        tb_rows = tb.rearrange("(p t) v -> t p v", t=PACK)

        def scale_rows(scales, low):
            return scales[0].rearrange("(b q r) n -> q r b n", b=2, q=2)[low].bitcast(I32)

        nc.sync.dma_start(
            xs_stage[:].bitcast(I32).rearrange("r (q n) -> r q n", q=4),
            xt_scales[0].rearrange("(q r) n -> r q n", r=4).bitcast(I32),
        )
        nc.sync.dma_start(l1[:], offs)
        nc.sync.dma_start(w_raw[:].bitcast(I32), w_words[0].rearrange("p n t -> p (n t)").bitcast(I32))
        for low in range(2):
            nc.sync.dma_start(
                wsc_raw[32 * low : 32 * low + 4, :].bitcast(I32).rearrange("r (b n) -> r b n", b=2),
                scale_rows(w_scales, low),
            )
        nc.sync.dma_start(x_words[:].bitcast(I32), xt_words[0].bitcast(I32))
        nc.sync.dma_start(l2[:], offs2)
        nc.sync.dma_start(tb_sb[0][:], tb_rows[0])
        nc.sync.dma_start(sa_sb[:], sa.rearrange("(p t) o -> p (t o)", t=PACK))
        nc.sync.dma_start(l3[:], offs3)
        nc.sync.dma_start(sb_sb[:], sb.rearrange("(p t) o -> p (t o)", t=PACK))
        nc.sync.dma_start(l4[:], offs4)
        nc.sync.dma_start(tb_sb[1][:], tb_rows[1])
        nc.sync.dma_start(tb_sb[2][:], tb_rows[2])
        for which, scales in enumerate((ws_scales, wb_scales)):
            for low in range(2):
                nc.sync.dma_start(
                    osc[32 * low : 32 * low + 4, :].bitcast(I32).rearrange("r (b w n) -> r b w n", b=2, w=2)[:, :, which, :],
                    scale_rows(scales, low),
                )
        nc.sync.dma_start(tb_sb[3][:], tb_rows[3])
        nc.sync.dma_start(ws_sb[:].bitcast(I32), ws_words[0].rearrange("p n t -> p (n t)").bitcast(I32))
        nc.sync.dma_start(wb_sb[:].bitcast(I32), wb_words[0].bitcast(I32))

        for q in range(4):
            nc.vector.tensor_copy(
                out=xs_plane[32 * q : 32 * q + 4, :].bitcast(I32),
                in_=xs_stage[:, q * T : (q + 1) * T].bitcast(I32),
            )
        nc.scalar.copy(
            out=w_dealt[:].rearrange("p (t m) -> p m t", t=PACK),
            in_=w_raw[:].rearrange("p (m t) -> p m t", t=PACK),
        )
        xg_words = sbuf("xg_words", [P, J], U16)
        xg_scales = sbuf("xg_scales", [P, J], U8)
        nc.vector.tensor_copy(xg_words[:], x_words[:].indirect(l1[:]))
        nc.vector.tensor_copy(xg_scales[:], xs_plane[:].indirect(l1[:]))
        nc.vector.tensor_copy(out=wsc_raw[64:128, 0:R].bitcast(I32), in_=wsc_raw[0:64, R : 2 * R].bitcast(I32))
        nc.vector.tensor_copy(
            out=wsc_dealt[:].rearrange("p (t m) -> p m t", t=PACK),
            in_=wsc_raw[:, 0:R].rearrange("p (m t) -> p m t", t=PACK),
        )

        a_ps = [psum.tile([P, 2, J], F32, name="a%d" % u) for u in range(2)]
        for t in range(PACK):
            cols = slice(t * P, (t + 1) * P)
            nc.tensor.matmul_mx(
                out=a_ps[t // 2][:, t % 2, :],
                lhsT=w_dealt[:, cols].bitcast(E4M3), lhsT_scale=wsc_dealt[:, cols],
                rhs=xg_words[:].bitcast(E2M1), rhs_scale=xg_scales[:],
                start=True, stop=True,
            )

        xs_words = sbuf("xs_words", [P, J], U16)
        xs_scales = sbuf("xs_scales", [P, J], U8)
        nc.vector.tensor_copy(xs_words[:], x_words[:].indirect(l4[:]))
        nc.vector.tensor_copy(xs_scales[:], xs_plane[:].indirect(l4[:]))

        upper = [sbuf("upper%d" % u, [P, 2, J], F32) for u in range(2)]
        lower01 = sbuf("lower01", [P, 2, J], F32)
        lower23 = [sbuf("lower23_%d" % h, [P, 2, HALF], F32) for h in range(2)]
        cut = [sbuf("cut%d" % u, [P, 2, J], F32) for u in range(2)]
        hid = sbuf("hid", [P, J, PACK], BF16)

        def fetch(dst, t, lst, step):
            nc.scalar.activation(out=dst, in_=tb_sb[t][:].indirect(lst), func=COPY, scale=step[:, t : t + 1])

        for t in range(2):
            fetch(upper[0][:, t, :], t, l2[:], sa_sb)
            fetch(lower01[:, t, :], t, l3[:], sb_sb)
        nc.vector.tensor_tensor(cut[0][:], a_ps[0][:], upper[0][:], ALU.min)
        nc.vector.tensor_tensor(
            hid[:, :, 0:2], cut[0][:].rearrange("p t j -> p j t"), lower01[:].rearrange("p t j -> p j t"), ALU.max
        )
        nc.vector.tensor_copy(out=osc[64:128, 0 : 2 * N].bitcast(I32), in_=osc[0:64, 2 * N : 4 * N].bitcast(I32))

        y_ps = [[psum.tile([P, HALF], F32, name="y%d%d" % (h, m)) for m in range(2)] for h in range(2)]
        for h in range(2):
            js = slice(h * HALF, (h + 1) * HALF)
            for m in range(2):
                nc.tensor.matmul_mx(
                    out=y_ps[h][m][:],
                    lhsT=ws_sb[:, m * P : (m + 1) * P].bitcast(E4M3), lhsT_scale=osc[:, m * P : (m + 1) * P],
                    rhs=xs_words[:, js].bitcast(E2M1), rhs_scale=xs_scales[:, js],
                    start=True, stop=False,
                )

        for t in range(2, 4):
            fetch(upper[1][:, t - 2, :], t, l2[:], sa_sb)
            nc.vector.tensor_tensor(cut[1][:, t - 2, :], a_ps[1][:, t - 2, :], upper[1][:, t - 2, :], ALU.min)
            for h in range(2):
                fetch(lower23[h][:, t - 2, :], t, l3[:, h * LIST_COLS // 2 : (h + 1) * LIST_COLS // 2], sb_sb)

        hid_codes = sbuf("hid_codes", [P, J], U32)
        hid_scales = sbuf("hid_scales", [P, J], U8)
        for h in range(2):
            js = slice(h * HALF, (h + 1) * HALF)
            nc.vector.tensor_tensor(
                hid[:, js, 2:4], cut[1][:, :, js].rearrange("p t j -> p j t"),
                lower23[h][:].rearrange("p t j -> p j t"), ALU.max,
            )
        out_rows = out.rearrange("(m p) j -> p m j", p=P)
        for h in range(2):
            js = slice(h * HALF, (h + 1) * HALF)
            nc.vector.quantize_mx(
                out=hid_codes[:, js].bitcast(E5M2), scales=hid_scales[:, js],
                in_=hid[:, js, :].rearrange("p j t -> p (j t)"),
            )
            for m in range(2):
                nc.tensor.matmul_mx(
                    out=y_ps[h][m][:],
                    lhsT=wb_sb[:, 2 * m * P : 2 * (m + 1) * P].bitcast(E2M1),
                    lhsT_scale=osc[:, N + m * P : N + (m + 1) * P],
                    rhs=hid_codes[:, js].bitcast(E5M2), rhs_scale=hid_scales[:, js],
                    start=False, stop=True,
                )
            y_sb = sbuf("y_sb%d" % h, [P, 2, HALF], F32)
            nc.scalar.copy(out=y_sb[:, 0, :], in_=y_ps[h][0][:])
            if h == 0:
                nc.scalar.copy(out=y_sb[:, 1, :], in_=y_ps[h][1][:])
            else:
                nc.vector.tensor_copy(out=y_sb[:, 1, :], in_=y_ps[h][1][:])
            nc.sync.dma_start(out_rows[:, :, js], y_sb[:])
